import numpy as np
import ml_dtypes


def mxq(x, axis, fmt="e4m3"):
    dtype, down = {"e4m3": (ml_dtypes.float8_e4m3fn, 7), "e5m2": (ml_dtypes.float8_e5m2, 14)}[fmt]
    v = np.moveaxis(np.asarray(x, np.float32).astype(ml_dtypes.bfloat16).astype(np.float64), axis, -1)
    blocks = v.reshape(v.shape[:-1] + (-1, 32))
    amax = np.abs(blocks).max(-1, keepdims=True)
    byte = np.maximum(np.where(amax > 0, np.frexp(amax)[1] - 1 + 127, 0) - down, 1)
    scale = np.exp2(byte - 127.0)
    codes = (blocks / scale).astype(np.float32).astype(dtype).astype(np.float64)
    return np.moveaxis((codes * scale).reshape(v.shape), -1, axis)


WIDE = False


def mx_kscale(k):
    if not WIDE:
        return np.ones(k)
    levels = np.array([30, -30])
    if k % 512:
        return np.exp2(np.random.permutation(np.resize(levels, k // 32))).repeat(32)
    a = np.empty((k // 512, 16))
    for p in range(k // 512):
        a[p, :8] = np.random.permutation(np.resize(levels, 8))
        for g in range(8):
            far = levels[np.abs(levels - a[p, g]) >= 10]
            a[p, g + 8] = far[np.random.randint(len(far))]
    return np.exp2(a.ravel()).repeat(32)


def f64(x):
    return np.asarray(x).astype(np.float64)


def striped(idx):
    return np.tile(np.asarray(idx).reshape(-1, 16).T, (8, 1)).astype(np.uint16)


def unstriped(offs):
    return offs[:16].T.reshape(-1).astype(np.int64)


E2M1 = np.array([0.0, 0.5, 1.0, 1.5, 2.0, 3.0, 4.0, 6.0, -0.0, -0.5, -1.0, -1.5, -2.0, -3.0, -4.0, -6.0])


def pack_weight(w, fmt):
    k, n = w.shape
    w = f64(np.asarray(w, np.float32).astype(ml_dtypes.bfloat16)).reshape(k // 32, 32, n)
    amax = np.abs(w).max(1)
    if fmt in ("e4m3", "e5m2"):
        byte = np.frexp(amax)[1] - 1 + 127 - (7 if fmt == "e4m3" else 14)
    else:
        mant, ex = np.frexp(amax / 6.0)
        byte = np.where(mant > 0.5, ex, ex - 1) + 127
    byte = np.clip(np.where(amax > 0, byte, 1), 1, 254)
    scaled = (w * np.exp2(127.0 - byte)[:, None, :]).reshape(k, n).astype(np.float32)
    by_word = np.ascontiguousarray(scaled.reshape(k // 512, 128, 4, n).transpose(0, 1, 3, 2))
    if fmt in ("e4m3", "e5m2"):
        words = by_word.astype(ml_dtypes.float8_e4m3fn if fmt == "e4m3" else ml_dtypes.float8_e5m2).view(np.uint8)
    else:
        c = by_word.astype(ml_dtypes.float4_e2m1fn).view(np.uint8) & 0xF
        words = (c[..., 0::2] | (c[..., 1::2] << 4)).reshape(k // 512, 128, 2 * n)
    return np.ascontiguousarray(words), np.ascontiguousarray(byte.astype(np.uint8).reshape(k // 512, 16, n))


def unpack_weight(words, scales, fmt):
    g, _, n = scales.shape
    words = np.ascontiguousarray(words).reshape(g, 128, n, -1)
    if fmt in ("e4m3", "e5m2"):
        vals = words.view(ml_dtypes.float8_e4m3fn if fmt == "e4m3" else ml_dtypes.float8_e5m2).astype(np.float64)
    else:
        nib = np.empty((g, 128, n, 4), np.uint8)
        nib[..., 0::2] = words & 0xF
        nib[..., 1::2] = words >> 4
        vals = E2M1[nib]
    vals = vals * np.repeat(np.exp2(scales.astype(np.float64) - 127.0), 8, axis=1)[..., None]
    return vals.transpose(0, 1, 3, 2).reshape(g * 512, n)


K, F, T, Z, J, R, C, V, O, N, S = 512, 512, 1024, 1024, 256, 512, 512, 1024, 256, 256, 1024


def setup_inputs():
    n = np.random.standard_normal
    idx = np.random.permutation(T)[:J]
    idx2 = np.random.permutation(Z)[:J]
    idx3 = np.random.permutation(C)[:J]
    idx4 = np.random.permutation(V)[:C]
    idx5 = np.random.permutation(C)[:O]
    idx6 = np.random.permutation(S)[:N]
    fk = mx_kscale(K)
    fr = mx_kscale(R)
    ff = mx_kscale(F)
    xtp = pack_weight(n((K, T)) / fk[:, None], "e2m1")
    wp = pack_weight(n((K, R)) * 1 / np.sqrt(K) * fk[:, None] * fr, "e5m2")
    xop = pack_weight(n((F, Z)) / ff[:, None], "e5m2")
    w0p = pack_weight(n((F, R)) * 1 / np.sqrt(F) * ff[:, None] * fr, "e4m3")
    vsp = pack_weight(n((R, S)) * 1 / np.sqrt(R) / fr[:, None], "e4m3")
    return {
        "xt_words": xtp[0],
        "xt_scales": xtp[1],
        "w_words": wp[0],
        "w_scales": wp[1],
        "xo_words": xop[0],
        "xo_scales": xop[1],
        "w0_words": w0p[0],
        "w0_scales": w0p[1],
        "tb": (n((R, V)) * 0.8 * fr[:, None]).astype(np.float32),
        "vs_words": vsp[0],
        "vs_scales": vsp[1],
        "offs": striped(idx),
        "offs2": striped(idx2),
        "offs3": striped(idx3),
        "offs4": striped(idx4),
        "offs5": striped(idx5),
        "offs6": striped(idx6),
    }


def reference(xt_words, xt_scales, w_words, w_scales, xo_words, xo_scales, w0_words, w0_scales, tb, vs_words, vs_scales, offs, offs2, offs3, offs4, offs5, offs6):
    idx = unstriped(offs)
    idx2 = unstriped(offs2)
    idx3 = unstriped(offs3)
    idx4 = unstriped(offs4)
    idx5 = unstriped(offs5)
    idx6 = unstriped(offs6)
    xtu = unpack_weight(xt_words, xt_scales, "e2m1")
    wu = unpack_weight(w_words, w_scales, "e5m2")
    xou = unpack_weight(xo_words, xo_scales, "e5m2")
    w0u = unpack_weight(w0_words, w0_scales, "e4m3")
    vsu = unpack_weight(vs_words, vs_scales, "e4m3")
    xtidxg = xtu[:, idx]
    xoidx2g = xou[:, idx2]
    a = wu.T @ xtidxg + w0u.T @ xoidx2g
    pw = np.zeros((R, C))
    pw[:, idx3] = a
    pg = np.abs(pw - f64(tb)[:, idx4])
    hid = pg[:, idx5]
    vsidx6g = vsu[:, idx6]
    hidq = mxq(hid, 0, "e5m2")
    y = vsidx6g.T @ hidq
    return y

@@ -1,0 +1,192 @@
+from contextlib import ExitStack
+
+import concourse.mybir as mybir
+
+K, F, T, Z, J, R, C, V, O, N, S = 512, 512, 1024, 1024, 256, 512, 512, 1024, 256, 256, 1024
+FLOPS = 2 * K * R * J + 2 * F * R * J + 2 * R * N * O
+
+P = 128
+PACK = 4
+F32 = mybir.dt.float32
+BF16 = mybir.dt.bfloat16
+I32 = mybir.dt.int32
+U32 = mybir.dt.uint32
+U16 = mybir.dt.uint16
+U8 = mybir.dt.uint8
+E4M3 = mybir.dt.float8_e4m3fn_x4
+E5M2 = mybir.dt.float8_e5m2_x4
+E2M1 = mybir.dt.float4_e2m1fn_x4
+ACT = mybir.ActivationFunctionType
+ALU = mybir.AluOpType
+
+
+def tile_list_stampedtable_bank_store_plain_kernel(
+    tc, xt_words, xt_scales, w_words, w_scales, xo_words, xo_scales, w0_words, w0_scales, tb,
+    vs_words, vs_scales, offs, offs2, offs3, offs4, offs5, offs6, out,
+):
+    nc = tc.nc
+    with ExitStack() as ctx:
+        lists = ctx.enter_context(tc.tile_pool(name="lists", bufs=1))
+        sb = ctx.enter_context(tc.tile_pool(name="sb", bufs=1))
+        ps = ctx.enter_context(tc.psum_pool(name="ps", bufs=1))
+
+        def load_list(src, name):
+            tile = lists.tile([P, src.shape[1]], U16, name=name)
+            nc.sync.dma_start(tile[:], src)
+            return tile
+
+        def load_words(src, name):
+            tile = sb.tile([P, src.shape[2]], U32, name=name, align_bytes=64)
+            nc.sync.dma_start(tile[:].bitcast(I32), src[0].rearrange("p n t -> p (n t)").bitcast(I32))
+            return tile
+
+        def zeroed_bytes(width, name):
+            tile = sb.tile([P, width], U8, name=name, align_bytes=64)
+            nc.vector.memset(tile[:].bitcast(I32), 0)
+            return tile
+
+        def load_scales(queue, plane, src):
+            for q in range(4):
+                queue.dma_start(plane[32 * q : 32 * q + 4, :].bitcast(I32), src[0, 4 * q : 4 * q + 4, :].bitcast(I32))
+
+        def gather(window, idx, dtype, name):
+            tile = sb.tile([P, 16 * idx.shape[1]], dtype, name=name, align_bytes=64)
+            nc.vector.tensor_copy(tile[:], window[:].indirect(idx[:]))
+            return tile
+
+        xt_s = zeroed_bytes(T, "xt_s")
+        xo_s = zeroed_bytes(Z, "xo_s")
+        ww_s = zeroed_bytes(2 * R, "ww_s")
+        vs_s = zeroed_bytes(S, "vs_s")
+
+        tb_rows = tb.rearrange("(p t) v -> p t v", t=PACK)
+        tbt = [sb.tile([P, V], F32, name=f"tb{t}") for t in range(PACK)]
+        l1 = load_list(offs, "l1")
+        l2 = load_list(offs2, "l2")
+        xt_w = sb.tile([P, T], U16, name="xt_w", align_bytes=64)
+        nc.sync.dma_start(xt_w[:].bitcast(I32), xt_words[0].bitcast(I32))
+        xo_w = load_words(xo_words, "xo_w")
+        load_scales(nc.scalar, xt_s, xt_scales)
+        load_scales(nc.gpsimd, ww_s[:, R:], w0_scales)
+        l4 = load_list(offs4, "l4")
+        nc.sync.dma_start(tbt[0][:], tb_rows[:, 0, :])
+        w_w = load_words(w_words, "w_w")
+        w0_w = load_words(w0_words, "w0_w")
+        load_scales(nc.scalar, xo_s, xo_scales)
+        load_scales(nc.scalar, ww_s[:, :R], w_scales)
+        nc.sync.dma_start(tbt[1][:], tb_rows[:, 1, :])
+        l3 = load_list(offs3, "l3")
+        nc.sync.dma_start(tbt[2][:], tb_rows[:, 2, :])
+        l6 = load_list(offs6, "l6")
+        vs_w = load_words(vs_words, "vs_w")
+        nc.sync.dma_start(tbt[3][:], tb_rows[:, 3, :])
+        l5 = load_list(offs5, "l5")
+        load_scales(nc.gpsimd, vs_s, vs_scales)
+
+        pw = [sb.tile([P, C], F32, name=f"pw{t}") for t in range(PACK)]
+        for t in range(PACK):
+            nc.vector.memset(pw[t][:], 0.0)
+
+        xt_gw = gather(xt_w, l1, U16, "xt_gw")
+        xo_gw = gather(xo_w, l2, U32, "xo_gw")
+        xt_gs = gather(xt_s, l1, U8, "xt_gs")
+        xo_gs = gather(xo_s, l2, U8, "xo_gs")
+
+        w_d = sb.tile([P, R], U32, name="w_d", align_bytes=64)
+        w0_d = sb.tile([P, R], U32, name="w0_d", align_bytes=64)
+        for src, dst in ((w_w, w_d), (w0_w, w0_d)):
+            nc.vector.tensor_copy(
+                dst[:].bitcast(I32).rearrange("p (t m) -> p t m", t=PACK), src[:].bitcast(I32).rearrange("p (m t) -> p t m", t=PACK)
+            )
+        ww_d = sb.tile([P, 2 * R], U8, name="ww_d", align_bytes=64)
+        nc.vector.tensor_copy(
+            ww_d[:].rearrange("p (s t m) -> p s t m", s=2, t=PACK), ww_s[:].rearrange("p (s m t) -> p s t m", s=2, t=PACK)
+        )
+
+        tbg = [sb.tile([P, C], F32, name=f"tbg{t}") for t in range(PACK - 1)]
+
+        def tb_gather(t):
+            nc.scalar.activation(tbg[t][:], tbt[t][:].indirect(l4[:]), ACT.Copy)
+
+        tb_gather(0)
+        tb_gather(1)
+
+        accs = []
+        a_sb = [sb.tile([P, J], F32, name=f"a{t}") for t in range(PACK)]
+        for t in range(PACK):
+            acc = ps.tile([P, J], F32, name=f"acc{t}")
+            cols = slice(t * P, (t + 1) * P)
+            cols0 = slice(R + t * P, R + (t + 1) * P)
+            nc.tensor.matmul_mx(
+                acc[:], lhsT=w_d[:, cols].bitcast(E5M2), lhsT_scale=ww_d[:, cols],
+                rhs=xt_gw[:].bitcast(E2M1), rhs_scale=xt_gs[:], start=True, stop=False,
+            )
+            nc.tensor.matmul_mx(
+                acc[:], lhsT=w0_d[:, cols].bitcast(E4M3), lhsT_scale=ww_d[:, cols0],
+                rhs=xo_gw[:].bitcast(E5M2), rhs_scale=xo_gs[:], start=False, stop=True,
+            )
+            accs.append(acc)
+
+        diff = [sb.tile([P, C], F32, name=f"diff{t}") for t in range(PACK)]
+        pg = [sb.tile([P, C], F32, name=f"pg{t}") for t in range(PACK)]
+        hid = sb.tile([P, O, PACK], BF16, name="hid", align_bytes=64)
+
+        def scatter_v(t):
+            nc.vector.tensor_copy(pw[t][:].indirect(l3[:]), a_sb[t][:])
+
+        def scatter_s(t):
+            nc.scalar.activation(pw[t][:].indirect(l3[:]), a_sb[t][:], ACT.Copy)
+
+        def sub(t):
+            nc.vector.tensor_tensor(diff[t][:], pw[t][:], tbg[t][:], ALU.subtract)
+
+        def magnitude(t):
+            nc.scalar.activation(pg[t][:], diff[t][:], ACT.Abs)
+
+        def read(t):
+            nc.vector.tensor_copy(hid[:, :, t], pg[t][:].indirect(l5[:]))
+
+        def fused(t):
+            nc.vector.tensor_tensor(diff[t][:], tbt[t][:].indirect(l4[:]), pw[t][:], ALU.subtract)
+
+        nc.vector.tensor_copy(a_sb[0][:], accs[0][:])
+        scatter_v(0)
+        nc.scalar.copy(a_sb[1][:], accs[1][:])
+        scatter_s(1)
+        sub(0)
+        nc.scalar.copy(a_sb[2][:], accs[2][:])
+        nc.scalar.copy(a_sb[3][:], accs[3][:])
+        magnitude(0)
+        sub(1)
+        scatter_s(3)
+        scatter_v(2)
+        magnitude(1)
+        tb_gather(2)
+        read(0)
+        fused(3)
+        magnitude(3)
+        sub(2)
+        read(1)
+        magnitude(2)
+        vs_gw = gather(vs_w, l6, U32, "vs_gw")
+        vs_gs = gather(vs_s, l6, U8, "vs_gs")
+        read(3)
+        read(2)
+
+        hq_w = sb.tile([P, O], U32, name="hq_w", align_bytes=64)
+        hq_s = sb.tile([P, O], U8, name="hq_s", align_bytes=64)
+        nc.vector.quantize_mx(hq_w[:].bitcast(E5M2), hq_s[:], hid[:].rearrange("p o t -> p (o t)"))
+
+        for h in range(N // P):
+            res = ps.tile([P, O], F32, name=f"res{h}")
+            cols = slice(h * P, (h + 1) * P)
+            nc.tensor.matmul_mx(
+                res[:], lhsT=vs_gw[:, cols].bitcast(E4M3), lhsT_scale=vs_gs[:, cols],
+                rhs=hq_w[:].bitcast(E5M2), rhs_scale=hq_s[:], start=True, stop=True,
+            )
+            y = sb.tile([P, O], F32, name=f"y{h}")
+            if h == 0:
+                nc.scalar.copy(y[:], res[:])
+            else:
+                nc.vector.tensor_copy(y[:], res[:])
+            nc.sync.dma_start(out[cols, :], y[:])

@@ -30,23 +30,19 @@ def tile_list_stampedtable_bank_store_plain_kernel(
         sb = ctx.enter_context(tc.tile_pool(name="sb", bufs=1))
         ps = ctx.enter_context(tc.psum_pool(name="ps", bufs=1))
 
-        def load_list(src, name):
-            tile = lists.tile([P, src.shape[1]], U16, name=name)
-            nc.sync.dma_start(tile[:], src)
-            return tile
-
-        def load_words(src, name):
-            tile = sb.tile([P, src.shape[2]], U32, name=name, align_bytes=64)
-            nc.sync.dma_start(tile[:].bitcast(I32), src[0].rearrange("p n t -> p (n t)").bitcast(I32))
-            return tile
+        def list_tile(src, name):
+            return lists.tile([P, src.shape[1]], U16, name=name)
 
         def zeroed_bytes(width, name):
             tile = sb.tile([P, width], U8, name=name, align_bytes=64)
             nc.vector.memset(tile[:].bitcast(I32), 0)
             return tile
 
-        def load_scales(queue, plane, src):
-            for q in range(4):
+        def load_words(queue, tile, src):
+            queue.dma_start(tile[:].bitcast(I32), src[0].rearrange("p n t -> p (n t)").bitcast(I32))
+
+        def load_scales(queue, plane, src, quads=range(4)):
+            for q in quads:
                 queue.dma_start(plane[32 * q : 32 * q + 4, :].bitcast(I32), src[0, 4 * q : 4 * q + 4, :].bitcast(I32))
 
         def gather(window, idx, dtype, name):
@@ -54,124 +50,111 @@ def tile_list_stampedtable_bank_store_plain_kernel(
             nc.vector.tensor_copy(tile[:], window[:].indirect(idx[:]))
             return tile
 
+        def deal(src, dtype, view, name):
+            tile = sb.tile([P, R], dtype, name=name, align_bytes=64)
+            nc.vector.tensor_copy(
+                tile[:].bitcast(view).rearrange("p (t m) -> p t m", t=PACK),
+                src[:].bitcast(view).rearrange("p (m t) -> p t m", t=PACK),
+            )
+            return tile
+
         xt_s = zeroed_bytes(T, "xt_s")
         xo_s = zeroed_bytes(Z, "xo_s")
-        ww_s = zeroed_bytes(2 * R, "ww_s")
+        w_s = zeroed_bytes(R, "w_s")
+        w0_s = zeroed_bytes(R, "w0_s")
         vs_s = zeroed_bytes(S, "vs_s")
-
-        tb_rows = tb.rearrange("(p t) v -> p t v", t=PACK)
-        tbt = [sb.tile([P, V], F32, name=f"tb{t}") for t in range(PACK)]
-        l1 = load_list(offs, "l1")
-        l2 = load_list(offs2, "l2")
+        l1, l2, l3 = list_tile(offs, "l1"), list_tile(offs2, "l2"), list_tile(offs3, "l3")
+        l4, l5, l6 = list_tile(offs4, "l4"), list_tile(offs5, "l5"), list_tile(offs6, "l6")
         xt_w = sb.tile([P, T], U16, name="xt_w", align_bytes=64)
+        xo_w = sb.tile([P, Z], U32, name="xo_w", align_bytes=64)
+        w_w = sb.tile([P, R], U32, name="w_w", align_bytes=64)
+        w0_w = sb.tile([P, R], U32, name="w0_w", align_bytes=64)
+        vs_w = sb.tile([P, S], U32, name="vs_w", align_bytes=64)
+        tb_rows = tb.rearrange("(p t) v -> p t v", t=PACK)
+        tbt = [sb.tile([P, V], F32, name=f"tb{t}", tag=f"tb{t}", align_bytes=64) for t in range(PACK)]
+
+        nc.sync.dma_start(l1[:], offs)
         nc.sync.dma_start(xt_w[:].bitcast(I32), xt_words[0].bitcast(I32))
-        xo_w = load_words(xo_words, "xo_w")
-        load_scales(nc.scalar, xt_s, xt_scales)
-        load_scales(nc.gpsimd, ww_s[:, R:], w0_scales)
-        l4 = load_list(offs4, "l4")
+        load_scales(nc.sync, xt_s, xt_scales)
+        nc.sync.dma_start(l2[:], offs2)
+        load_words(nc.sync, xo_w, xo_words)
+        load_scales(nc.sync, xo_s, xo_scales)
+        load_words(nc.sync, w_w, w_words)
+        load_scales(nc.sync, w_s, w_scales)
+        load_words(nc.sync, w0_w, w0_words)
+        load_scales(nc.sync, w0_s, w0_scales)
+        nc.sync.dma_start(l3[:], offs3)
         nc.sync.dma_start(tbt[0][:], tb_rows[:, 0, :])
-        w_w = load_words(w_words, "w_w")
-        w0_w = load_words(w0_words, "w0_w")
-        load_scales(nc.scalar, xo_s, xo_scales)
-        load_scales(nc.scalar, ww_s[:, :R], w_scales)
+        nc.sync.dma_start(l4[:], offs4)
         nc.sync.dma_start(tbt[1][:], tb_rows[:, 1, :])
-        l3 = load_list(offs3, "l3")
+        nc.sync.dma_start(l6[:], offs6)
+        load_words(nc.sync, vs_w, vs_words)
+        load_scales(nc.sync, vs_s, vs_scales)
         nc.sync.dma_start(tbt[2][:], tb_rows[:, 2, :])
-        l6 = load_list(offs6, "l6")
-        vs_w = load_words(vs_words, "vs_w")
         nc.sync.dma_start(tbt[3][:], tb_rows[:, 3, :])
-        l5 = load_list(offs5, "l5")
-        load_scales(nc.gpsimd, vs_s, vs_scales)
+        nc.sync.dma_start(l5[:], offs5)
 
         pw = [sb.tile([P, C], F32, name=f"pw{t}") for t in range(PACK)]
         for t in range(PACK):
             nc.vector.memset(pw[t][:], 0.0)
 
         xt_gw = gather(xt_w, l1, U16, "xt_gw")
-        xo_gw = gather(xo_w, l2, U32, "xo_gw")
         xt_gs = gather(xt_s, l1, U8, "xt_gs")
-        xo_gs = gather(xo_s, l2, U8, "xo_gs")
-
+        xo_gw = gather(xo_w, l2, U32, "xo_gw")
         w_d = sb.tile([P, R], U32, name="w_d", align_bytes=64)
-        w0_d = sb.tile([P, R], U32, name="w0_d", align_bytes=64)
-        for src, dst in ((w_w, w_d), (w0_w, w0_d)):
-            nc.vector.tensor_copy(
-                dst[:].bitcast(I32).rearrange("p (t m) -> p t m", t=PACK), src[:].bitcast(I32).rearrange("p (m t) -> p t m", t=PACK)
-            )
-        ww_d = sb.tile([P, 2 * R], U8, name="ww_d", align_bytes=64)
-        nc.vector.tensor_copy(
-            ww_d[:].rearrange("p (s t m) -> p s t m", s=2, t=PACK), ww_s[:].rearrange("p (s m t) -> p s t m", s=2, t=PACK)
-        )
+        nc.scalar.copy(w_d[:].rearrange("p (t m) -> p t m", t=PACK), w_w[:].rearrange("p (m t) -> p t m", t=PACK))
+        xo_gs = gather(xo_s, l2, U8, "xo_gs")
+        w_ds = deal(w_s, U8, U8, "w_ds")
+        w0_d = deal(w0_w, U32, I32, "w0_d")
+        w0_ds = deal(w0_s, U8, U8, "w0_ds")
 
-        tbg = [sb.tile([P, C], F32, name=f"tbg{t}") for t in range(PACK - 1)]
-
-        def tb_gather(t):
-            nc.scalar.activation(tbg[t][:], tbt[t][:].indirect(l4[:]), ACT.Copy)
-
-        tb_gather(0)
-        tb_gather(1)
-
-        accs = []
+        tbg = [sb.tile([P, C], F32, name=f"tbg{t}") for t in range(PACK)]
         a_sb = [sb.tile([P, J], F32, name=f"a{t}") for t in range(PACK)]
-        for t in range(PACK):
-            acc = ps.tile([P, J], F32, name=f"acc{t}")
-            cols = slice(t * P, (t + 1) * P)
-            cols0 = slice(R + t * P, R + (t + 1) * P)
-            nc.tensor.matmul_mx(
-                acc[:], lhsT=w_d[:, cols].bitcast(E5M2), lhsT_scale=ww_d[:, cols],
-                rhs=xt_gw[:].bitcast(E2M1), rhs_scale=xt_gs[:], start=True, stop=False,
-            )
-            nc.tensor.matmul_mx(
-                acc[:], lhsT=w0_d[:, cols].bitcast(E4M3), lhsT_scale=ww_d[:, cols0],
-                rhs=xo_gw[:].bitcast(E5M2), rhs_scale=xo_gs[:], start=False, stop=True,
-            )
-            accs.append(acc)
-
         diff = [sb.tile([P, C], F32, name=f"diff{t}") for t in range(PACK)]
         pg = [sb.tile([P, C], F32, name=f"pg{t}") for t in range(PACK)]
         hid = sb.tile([P, O, PACK], BF16, name="hid", align_bytes=64)
+        acc = [ps.tile([P, J], F32, name=f"acc{t}") for t in range(PACK)]
+        vs_gw = sb.tile([P, N], U32, name="vs_gw", align_bytes=64)
+        vs_gs = sb.tile([P, N], U8, name="vs_gs", align_bytes=64)
 
-        def scatter_v(t):
-            nc.vector.tensor_copy(pw[t][:].indirect(l3[:]), a_sb[t][:])
 
-        def scatter_s(t):
-            nc.scalar.activation(pw[t][:].indirect(l3[:]), a_sb[t][:], ACT.Copy)
+        for t in range(PACK):
+            cols = slice(t * P, (t + 1) * P)
+            nc.tensor.matmul_mx(
+                acc[t][:], lhsT=w_d[:, cols].bitcast(E5M2), lhsT_scale=w_ds[:, cols],
+                rhs=xt_gw[:].bitcast(E2M1), rhs_scale=xt_gs[:], start=True, stop=False,
+            )
+            nc.tensor.matmul_mx(
+                acc[t][:], lhsT=w0_d[:, cols].bitcast(E4M3), lhsT_scale=w0_ds[:, cols],
+                rhs=xo_gw[:].bitcast(E5M2), rhs_scale=xo_gs[:], start=False, stop=True,
+            )
 
-        def sub(t):
-            nc.vector.tensor_tensor(diff[t][:], pw[t][:], tbg[t][:], ALU.subtract)
-
-        def magnitude(t):
-            nc.scalar.activation(pg[t][:], diff[t][:], ACT.Abs)
-
-        def read(t):
-            nc.vector.tensor_copy(hid[:, :, t], pg[t][:].indirect(l5[:]))
-
-        def fused(t):
-            nc.vector.tensor_tensor(diff[t][:], tbt[t][:].indirect(l4[:]), pw[t][:], ALU.subtract)
-
-        nc.vector.tensor_copy(a_sb[0][:], accs[0][:])
-        scatter_v(0)
-        nc.scalar.copy(a_sb[1][:], accs[1][:])
-        scatter_s(1)
-        sub(0)
-        nc.scalar.copy(a_sb[2][:], accs[2][:])
-        nc.scalar.copy(a_sb[3][:], accs[3][:])
-        magnitude(0)
-        sub(1)
-        scatter_s(3)
-        scatter_v(2)
-        magnitude(1)
-        tb_gather(2)
-        read(0)
-        fused(3)
-        magnitude(3)
-        sub(2)
-        read(1)
-        magnitude(2)
-        vs_gw = gather(vs_w, l6, U32, "vs_gw")
-        vs_gs = gather(vs_s, l6, U8, "vs_gs")
-        read(3)
-        read(2)
+        nc.scalar.copy(a_sb[0][:], acc[0][:])
+        nc.scalar.activation(pw[0][:].indirect(l3[:]), a_sb[0][:], ACT.Copy)
+        nc.vector.tensor_copy(a_sb[1][:], acc[1][:])
+        nc.scalar.activation(pw[1][:].indirect(l3[:]), a_sb[1][:], ACT.Copy)
+        nc.vector.tensor_copy(a_sb[2][:], acc[2][:])
+        nc.scalar.activation(pw[2][:].indirect(l3[:]), a_sb[2][:], ACT.Copy)
+        nc.vector.tensor_copy(a_sb[3][:], acc[3][:])
+        nc.scalar.activation(pw[3][:].indirect(l3[:]), a_sb[3][:], ACT.Copy)
+        nc.vector.tensor_copy(tbg[0][:], tbt[0][:].indirect(l4[:]))
+        nc.vector.tensor_tensor(diff[0][:], pw[0][:], tbg[0][:], ALU.subtract)
+        nc.vector.tensor_copy(tbg[1][:], tbt[1][:].indirect(l4[:]))
+        nc.vector.tensor_tensor(diff[1][:], pw[1][:], tbg[1][:], ALU.subtract)
+        nc.vector.tensor_copy(vs_gw[:], vs_w[:].indirect(l6[:]))
+        nc.vector.tensor_copy(vs_gs[:], vs_s[:].indirect(l6[:]))
+        nc.vector.tensor_tensor(diff[2][:], tbt[2][:].indirect(l4[:]), pw[2][:], ALU.subtract)
+        nc.vector.tensor_tensor(diff[3][:], tbt[3][:].indirect(l4[:]), pw[3][:], ALU.subtract)
+        nc.scalar.activation(pg[0][:], diff[0][:], ACT.Abs)
+        nc.scalar.activation(pg[1][:], diff[1][:], ACT.Abs)
+        nc.scalar.activation(pg[2][:], diff[2][:], ACT.Abs)
+        nc.scalar.activation(pg[3][:], diff[3][:], ACT.Abs)
+        planes = sb.tile([P, PACK, O], BF16, name="planes", tag="tb3", align_bytes=64)
+        nc.scalar.activation(planes[:, 0, :], pg[0][:].indirect(l5[:]), ACT.Copy)
+        nc.vector.tensor_copy(planes[:, 1, :], pg[1][:].indirect(l5[:]))
+        nc.vector.tensor_copy(planes[:, 2, :], pg[2][:].indirect(l5[:]))
+        nc.scalar.activation(planes[:, 3, :], pg[3][:].indirect(l5[:]), ACT.Copy)
+        nc.vector.tensor_copy(hid[:], planes[:].rearrange("p t o -> p o t"))
 
         hq_w = sb.tile([P, O], U32, name="hq_w", align_bytes=64)
         hq_s = sb.tile([P, O], U8, name="hq_s", align_bytes=64)

@@ -34,7 +34,7 @@ def tile_list_stampedtable_bank_store_plain_kernel(
             return lists.tile([P, src.shape[1]], U16, name=name)
 
         def zeroed_bytes(width, name):
-            tile = sb.tile([P, width], U8, name=name, align_bytes=64)
+            tile = sb.tile([P, width], U8, name=name, tag=name, align_bytes=64)
             nc.vector.memset(tile[:].bitcast(I32), 0)
             return tile
 
@@ -69,7 +69,7 @@ def tile_list_stampedtable_bank_store_plain_kernel(
         xo_w = sb.tile([P, Z], U32, name="xo_w", align_bytes=64)
         w_w = sb.tile([P, R], U32, name="w_w", align_bytes=64)
         w0_w = sb.tile([P, R], U32, name="w0_w", align_bytes=64)
-        vs_w = sb.tile([P, S], U32, name="vs_w", align_bytes=64)
+        vs_w = sb.tile([P, S], U32, name="vs_w", tag="vs_w", align_bytes=64)
         tb_rows = tb.rearrange("(p t) v -> p t v", t=PACK)
         tbt = [sb.tile([P, V], F32, name=f"tb{t}", tag=f"tb{t}", align_bytes=64) for t in range(PACK)]
 
@@ -78,20 +78,20 @@ def tile_list_stampedtable_bank_store_plain_kernel(
         load_scales(nc.sync, xt_s, xt_scales)
         nc.sync.dma_start(l2[:], offs2)
         load_words(nc.sync, xo_w, xo_words)
-        load_scales(nc.sync, xo_s, xo_scales)
         load_words(nc.sync, w_w, w_words)
         load_scales(nc.sync, w_s, w_scales)
         load_words(nc.sync, w0_w, w0_words)
+        load_scales(nc.sync, xo_s, xo_scales)
         load_scales(nc.sync, w0_s, w0_scales)
         nc.sync.dma_start(l3[:], offs3)
         nc.sync.dma_start(tbt[0][:], tb_rows[:, 0, :])
         nc.sync.dma_start(l4[:], offs4)
         nc.sync.dma_start(tbt[1][:], tb_rows[:, 1, :])
-        nc.sync.dma_start(l6[:], offs6)
-        load_words(nc.sync, vs_w, vs_words)
-        load_scales(nc.sync, vs_s, vs_scales)
         nc.sync.dma_start(tbt[2][:], tb_rows[:, 2, :])
         nc.sync.dma_start(tbt[3][:], tb_rows[:, 3, :])
+        nc.sync.dma_start(l6[:], offs6)
+        load_scales(nc.sync, vs_s, vs_scales)
+        load_words(nc.sync, vs_w, vs_words)
         nc.sync.dma_start(l5[:], offs5)
 
         pw = [sb.tile([P, C], F32, name=f"pw{t}") for t in range(PACK)]
@@ -103,15 +103,16 @@ def tile_list_stampedtable_bank_store_plain_kernel(
         xo_gw = gather(xo_w, l2, U32, "xo_gw")
         w_d = sb.tile([P, R], U32, name="w_d", align_bytes=64)
         nc.scalar.copy(w_d[:].rearrange("p (t m) -> p t m", t=PACK), w_w[:].rearrange("p (m t) -> p t m", t=PACK))
-        xo_gs = gather(xo_s, l2, U8, "xo_gs")
         w_ds = deal(w_s, U8, U8, "w_ds")
-        w0_d = deal(w0_w, U32, I32, "w0_d")
+        w0_d = sb.tile([P, R], U32, name="w0_d", align_bytes=64)
+        nc.scalar.copy(w0_d[:].rearrange("p (t m) -> p t m", t=PACK), w0_w[:].rearrange("p (m t) -> p t m", t=PACK))
+        xo_gs = gather(xo_s, l2, U8, "xo_gs")
         w0_ds = deal(w0_s, U8, U8, "w0_ds")
 
-        tbg = [sb.tile([P, C], F32, name=f"tbg{t}") for t in range(PACK)]
-        a_sb = [sb.tile([P, J], F32, name=f"a{t}") for t in range(PACK)]
-        diff = [sb.tile([P, C], F32, name=f"diff{t}") for t in range(PACK)]
-        pg = [sb.tile([P, C], F32, name=f"pg{t}") for t in range(PACK)]
+        tbg = {}
+        a_sb = [sb.tile([P, J], F32, name=f"a{t}", tag=f"a{t}", align_bytes=64) for t in range(PACK)]
+        diff = {}
+        pg = {}
         hid = sb.tile([P, O, PACK], BF16, name="hid", align_bytes=64)
         acc = [ps.tile([P, J], F32, name=f"acc{t}") for t in range(PACK)]
         vs_gw = sb.tile([P, N], U32, name="vs_gw", align_bytes=64)
@@ -132,29 +133,37 @@ def tile_list_stampedtable_bank_store_plain_kernel(
         nc.scalar.copy(a_sb[0][:], acc[0][:])
         nc.scalar.activation(pw[0][:].indirect(l3[:]), a_sb[0][:], ACT.Copy)
         nc.vector.tensor_copy(a_sb[1][:], acc[1][:])
-        nc.scalar.activation(pw[1][:].indirect(l3[:]), a_sb[1][:], ACT.Copy)
         nc.vector.tensor_copy(a_sb[2][:], acc[2][:])
-        nc.scalar.activation(pw[2][:].indirect(l3[:]), a_sb[2][:], ACT.Copy)
         nc.vector.tensor_copy(a_sb[3][:], acc[3][:])
+        nc.vector.tensor_copy(pw[1][:].indirect(l3[:]), a_sb[1][:])
+        nc.scalar.activation(pw[2][:].indirect(l3[:]), a_sb[2][:], ACT.Copy)
         nc.scalar.activation(pw[3][:].indirect(l3[:]), a_sb[3][:], ACT.Copy)
-        nc.vector.tensor_copy(tbg[0][:], tbt[0][:].indirect(l4[:]))
-        nc.vector.tensor_tensor(diff[0][:], pw[0][:], tbg[0][:], ALU.subtract)
-        nc.vector.tensor_copy(tbg[1][:], tbt[1][:].indirect(l4[:]))
-        nc.vector.tensor_tensor(diff[1][:], pw[1][:], tbg[1][:], ALU.subtract)
-        nc.vector.tensor_copy(vs_gw[:], vs_w[:].indirect(l6[:]))
-        nc.vector.tensor_copy(vs_gs[:], vs_s[:].indirect(l6[:]))
+        diff[0] = sb.tile([P, C], F32, name="diff0", tag="diff0", align_bytes=64)
+        nc.vector.tensor_tensor(diff[0][:], tbt[0][:].indirect(l4[:]), pw[0][:], ALU.subtract)
+        diff[1] = sb.tile([P, C], F32, name="diff1", tag="diff1", align_bytes=64)
+        nc.vector.tensor_tensor(diff[1][:], tbt[1][:].indirect(l4[:]), pw[1][:], ALU.subtract)
+        diff[2] = sb.tile([P, C], F32, name="diff2", tag="diff2", align_bytes=64)
         nc.vector.tensor_tensor(diff[2][:], tbt[2][:].indirect(l4[:]), pw[2][:], ALU.subtract)
+        diff[3] = sb.tile([P, C], F32, name="diff3", tag="diff3", align_bytes=64)
         nc.vector.tensor_tensor(diff[3][:], tbt[3][:].indirect(l4[:]), pw[3][:], ALU.subtract)
+        nc.vector.tensor_copy(vs_gs[:], vs_s[:].indirect(l6[:]))
+        nc.vector.tensor_copy(vs_gw[:], vs_w[:].indirect(l6[:]))
+        pg[0] = sb.tile([P, C], F32, name="pg0", tag="pg0", align_bytes=64)
         nc.scalar.activation(pg[0][:], diff[0][:], ACT.Abs)
+        pg[1] = sb.tile([P, C], F32, name="pg1", tag="pg1", align_bytes=64)
         nc.scalar.activation(pg[1][:], diff[1][:], ACT.Abs)
+        pg[2] = sb.tile([P, C], F32, name="pg2", tag="pg2", align_bytes=64)
         nc.scalar.activation(pg[2][:], diff[2][:], ACT.Abs)
+        pg[3] = sb.tile([P, C], F32, name="pg3", tag="pg3", align_bytes=64)
         nc.scalar.activation(pg[3][:], diff[3][:], ACT.Abs)
-        planes = sb.tile([P, PACK, O], BF16, name="planes", tag="tb3", align_bytes=64)
+        planes = sb.tile([P, PACK, O], BF16, name="planes", tag="diff0", align_bytes=64)
         nc.scalar.activation(planes[:, 0, :], pg[0][:].indirect(l5[:]), ACT.Copy)
-        nc.vector.tensor_copy(planes[:, 1, :], pg[1][:].indirect(l5[:]))
-        nc.vector.tensor_copy(planes[:, 2, :], pg[2][:].indirect(l5[:]))
-        nc.scalar.activation(planes[:, 3, :], pg[3][:].indirect(l5[:]), ACT.Copy)
-        nc.vector.tensor_copy(hid[:], planes[:].rearrange("p t o -> p o t"))
+        nc.scalar.activation(planes[:, 1, :], pg[1][:].indirect(l5[:]), ACT.Copy)
+        nc.scalar.activation(planes[:, 2, :], pg[2][:].indirect(l5[:]), ACT.Copy)
+        nc.vector.tensor_copy(planes[:, 3, :], pg[3][:].indirect(l5[:]))
+        woven = planes[:].rearrange("p t o -> p o t")
+        nc.vector.tensor_copy(hid[:, 80:, :], woven[:, 80:, :])
+        nc.scalar.copy(hid[:, :80, :], woven[:, :80, :])
 
         hq_w = sb.tile([P, O], U32, name="hq_w", align_bytes=64)
         hq_s = sb.tile([P, O], U8, name="hq_s", align_bytes=64)
@@ -169,7 +178,8 @@ def tile_list_stampedtable_bank_store_plain_kernel(
             )
             y = sb.tile([P, O], F32, name=f"y{h}")
             if h == 0:
-                nc.scalar.copy(y[:], res[:])
-            else:
                 nc.vector.tensor_copy(y[:], res[:])
-            nc.sync.dma_start(out[cols, :], y[:])
+                nc.sync.dma_start(out[cols, :], y[:])
+            else:
+                nc.scalar.copy(y[:], res[:])
+                nc.scalar.dma_start(out[cols, :], y[:])

from contextlib import ExitStack

import concourse.mybir as mybir

K, F, T, Z, J, R, C, V, O, N, S = 512, 512, 1024, 1024, 256, 512, 512, 1024, 256, 256, 1024
FLOPS = 2 * K * R * J + 2 * F * R * J + 2 * R * N * O

P = 128
PACK = 4
F32 = mybir.dt.float32
BF16 = mybir.dt.bfloat16
I32 = mybir.dt.int32
U32 = mybir.dt.uint32
U16 = mybir.dt.uint16
U8 = mybir.dt.uint8
E4M3 = mybir.dt.float8_e4m3fn_x4
E5M2 = mybir.dt.float8_e5m2_x4
E2M1 = mybir.dt.float4_e2m1fn_x4
ACT = mybir.ActivationFunctionType
ALU = mybir.AluOpType


def tile_list_stampedtable_bank_store_plain_kernel(
    tc, xt_words, xt_scales, w_words, w_scales, xo_words, xo_scales, w0_words, w0_scales, tb,
    vs_words, vs_scales, offs, offs2, offs3, offs4, offs5, offs6, out,
):
    nc = tc.nc
    with ExitStack() as ctx:
        lists = ctx.enter_context(tc.tile_pool(name="lists", bufs=1))
        sb = ctx.enter_context(tc.tile_pool(name="sb", bufs=1))
        ps = ctx.enter_context(tc.psum_pool(name="ps", bufs=1))

        def list_tile(src, name):
            return lists.tile([P, src.shape[1]], U16, name=name)

        def zeroed_bytes(width, name):
            tile = sb.tile([P, width], U8, name=name, tag=name, align_bytes=64)
            nc.vector.memset(tile[:].bitcast(I32), 0)
            return tile

        def load_words(queue, tile, src):
            queue.dma_start(tile[:].bitcast(I32), src[0].rearrange("p n t -> p (n t)").bitcast(I32))

        def load_scales(queue, plane, src, quads=range(4)):
            for q in quads:
                queue.dma_start(plane[32 * q : 32 * q + 4, :].bitcast(I32), src[0, 4 * q : 4 * q + 4, :].bitcast(I32))

        def gather(window, idx, dtype, name):
            tile = sb.tile([P, 16 * idx.shape[1]], dtype, name=name, align_bytes=64)
            nc.vector.tensor_copy(tile[:], window[:].indirect(idx[:]))
            return tile

        def deal(src, dtype, view, name):
            tile = sb.tile([P, R], dtype, name=name, align_bytes=64)
            nc.vector.tensor_copy(
                tile[:].bitcast(view).rearrange("p (t m) -> p t m", t=PACK),
                src[:].bitcast(view).rearrange("p (m t) -> p t m", t=PACK),
            )
            return tile

        xt_s = zeroed_bytes(T, "xt_s")
        xo_s = zeroed_bytes(Z, "xo_s")
        w_s = zeroed_bytes(R, "w_s")
        w0_s = zeroed_bytes(R, "w0_s")
        vs_s = zeroed_bytes(S, "vs_s")
        l1, l2, l3 = list_tile(offs, "l1"), list_tile(offs2, "l2"), list_tile(offs3, "l3")
        l4, l5, l6 = list_tile(offs4, "l4"), list_tile(offs5, "l5"), list_tile(offs6, "l6")
        xt_w = sb.tile([P, T], U16, name="xt_w", align_bytes=64)
        xo_w = sb.tile([P, Z], U32, name="xo_w", align_bytes=64)
        w_w = sb.tile([P, R], U32, name="w_w", align_bytes=64)
        w0_w = sb.tile([P, R], U32, name="w0_w", align_bytes=64)
        vs_w = sb.tile([P, S], U32, name="vs_w", tag="vs_w", align_bytes=64)
        tb_rows = tb.rearrange("(p t) v -> p t v", t=PACK)
        tbt = [sb.tile([P, V], F32, name=f"tb{t}", tag=f"tb{t}", align_bytes=64) for t in range(PACK)]

        nc.sync.dma_start(l1[:], offs)
        nc.sync.dma_start(xt_w[:].bitcast(I32), xt_words[0].bitcast(I32))
        load_scales(nc.sync, xt_s, xt_scales)
        nc.sync.dma_start(l2[:], offs2)
        load_words(nc.sync, xo_w, xo_words)
        load_words(nc.sync, w_w, w_words)
        load_scales(nc.sync, w_s, w_scales)
        load_words(nc.sync, w0_w, w0_words)
        load_scales(nc.sync, xo_s, xo_scales)
        load_scales(nc.sync, w0_s, w0_scales)
        nc.sync.dma_start(l3[:], offs3)
        nc.sync.dma_start(tbt[0][:], tb_rows[:, 0, :])
        nc.sync.dma_start(l4[:], offs4)
        nc.sync.dma_start(tbt[1][:], tb_rows[:, 1, :])
        nc.sync.dma_start(tbt[2][:], tb_rows[:, 2, :])
        nc.sync.dma_start(tbt[3][:], tb_rows[:, 3, :])
        nc.sync.dma_start(l6[:], offs6)
        load_scales(nc.sync, vs_s, vs_scales)
        load_words(nc.sync, vs_w, vs_words)
        nc.sync.dma_start(l5[:], offs5)

        pw = [sb.tile([P, C], F32, name=f"pw{t}") for t in range(PACK)]
        for t in range(PACK):
            nc.vector.memset(pw[t][:], 0.0)

        xt_gw = gather(xt_w, l1, U16, "xt_gw")
        xt_gs = gather(xt_s, l1, U8, "xt_gs")
        xo_gw = gather(xo_w, l2, U32, "xo_gw")
        w_d = sb.tile([P, R], U32, name="w_d", align_bytes=64)
        nc.scalar.copy(w_d[:].rearrange("p (t m) -> p t m", t=PACK), w_w[:].rearrange("p (m t) -> p t m", t=PACK))
        w_ds = deal(w_s, U8, U8, "w_ds")
        w0_d = sb.tile([P, R], U32, name="w0_d", align_bytes=64)
        nc.scalar.copy(w0_d[:].rearrange("p (t m) -> p t m", t=PACK), w0_w[:].rearrange("p (m t) -> p t m", t=PACK))
        xo_gs = gather(xo_s, l2, U8, "xo_gs")
        w0_ds = deal(w0_s, U8, U8, "w0_ds")

        tbg = {}
        a_sb = [sb.tile([P, J], F32, name=f"a{t}", tag=f"a{t}", align_bytes=64) for t in range(PACK)]
        diff = {}
        pg = {}
        hid = sb.tile([P, O, PACK], BF16, name="hid", align_bytes=64)
        acc = [ps.tile([P, J], F32, name=f"acc{t}") for t in range(PACK)]
        vs_gw = sb.tile([P, N], U32, name="vs_gw", align_bytes=64)
        vs_gs = sb.tile([P, N], U8, name="vs_gs", align_bytes=64)


        for t in range(PACK):
            cols = slice(t * P, (t + 1) * P)
            nc.tensor.matmul_mx(
                acc[t][:], lhsT=w_d[:, cols].bitcast(E5M2), lhsT_scale=w_ds[:, cols],
                rhs=xt_gw[:].bitcast(E2M1), rhs_scale=xt_gs[:], start=True, stop=False,
            )
            nc.tensor.matmul_mx(
                acc[t][:], lhsT=w0_d[:, cols].bitcast(E4M3), lhsT_scale=w0_ds[:, cols],
                rhs=xo_gw[:].bitcast(E5M2), rhs_scale=xo_gs[:], start=False, stop=True,
            )

        nc.scalar.copy(a_sb[0][:], acc[0][:])
        nc.scalar.activation(pw[0][:].indirect(l3[:]), a_sb[0][:], ACT.Copy)
        nc.vector.tensor_copy(a_sb[1][:], acc[1][:])
        nc.vector.tensor_copy(a_sb[2][:], acc[2][:])
        nc.vector.tensor_copy(a_sb[3][:], acc[3][:])
        nc.vector.tensor_copy(pw[1][:].indirect(l3[:]), a_sb[1][:])
        nc.scalar.activation(pw[2][:].indirect(l3[:]), a_sb[2][:], ACT.Copy)
        nc.scalar.activation(pw[3][:].indirect(l3[:]), a_sb[3][:], ACT.Copy)
        diff[0] = sb.tile([P, C], F32, name="diff0", tag="diff0", align_bytes=64)
        nc.vector.tensor_tensor(diff[0][:], tbt[0][:].indirect(l4[:]), pw[0][:], ALU.subtract)
        diff[1] = sb.tile([P, C], F32, name="diff1", tag="diff1", align_bytes=64)
        nc.vector.tensor_tensor(diff[1][:], tbt[1][:].indirect(l4[:]), pw[1][:], ALU.subtract)
        diff[2] = sb.tile([P, C], F32, name="diff2", tag="diff2", align_bytes=64)
        nc.vector.tensor_tensor(diff[2][:], tbt[2][:].indirect(l4[:]), pw[2][:], ALU.subtract)
        diff[3] = sb.tile([P, C], F32, name="diff3", tag="diff3", align_bytes=64)
        nc.vector.tensor_tensor(diff[3][:], tbt[3][:].indirect(l4[:]), pw[3][:], ALU.subtract)
        nc.vector.tensor_copy(vs_gs[:], vs_s[:].indirect(l6[:]))
        nc.vector.tensor_copy(vs_gw[:], vs_w[:].indirect(l6[:]))
        pg[0] = sb.tile([P, C], F32, name="pg0", tag="pg0", align_bytes=64)
        nc.scalar.activation(pg[0][:], diff[0][:], ACT.Abs)
        pg[1] = sb.tile([P, C], F32, name="pg1", tag="pg1", align_bytes=64)
        nc.scalar.activation(pg[1][:], diff[1][:], ACT.Abs)
        pg[2] = sb.tile([P, C], F32, name="pg2", tag="pg2", align_bytes=64)
        nc.scalar.activation(pg[2][:], diff[2][:], ACT.Abs)
        pg[3] = sb.tile([P, C], F32, name="pg3", tag="pg3", align_bytes=64)
        nc.scalar.activation(pg[3][:], diff[3][:], ACT.Abs)
        planes = sb.tile([P, PACK, O], BF16, name="planes", tag="diff0", align_bytes=64)
        nc.scalar.activation(planes[:, 0, :], pg[0][:].indirect(l5[:]), ACT.Copy)
        nc.scalar.activation(planes[:, 1, :], pg[1][:].indirect(l5[:]), ACT.Copy)
        nc.scalar.activation(planes[:, 2, :], pg[2][:].indirect(l5[:]), ACT.Copy)
        nc.vector.tensor_copy(planes[:, 3, :], pg[3][:].indirect(l5[:]))
        woven = planes[:].rearrange("p t o -> p o t")
        nc.vector.tensor_copy(hid[:, 80:, :], woven[:, 80:, :])
        nc.scalar.copy(hid[:, :80, :], woven[:, :80, :])

        hq_w = sb.tile([P, O], U32, name="hq_w", align_bytes=64)
        hq_s = sb.tile([P, O], U8, name="hq_s", align_bytes=64)
        nc.vector.quantize_mx(hq_w[:].bitcast(E5M2), hq_s[:], hid[:].rearrange("p o t -> p (o t)"))

        for h in range(N // P):
            res = ps.tile([P, O], F32, name=f"res{h}")
            cols = slice(h * P, (h + 1) * P)
            nc.tensor.matmul_mx(
                res[:], lhsT=vs_gw[:, cols].bitcast(E4M3), lhsT_scale=vs_gs[:, cols],
                rhs=hq_w[:].bitcast(E5M2), rhs_scale=hq_s[:], start=True, stop=True,
            )
            y = sb.tile([P, O], F32, name=f"y{h}")
            if h == 0:
                nc.vector.tensor_copy(y[:], res[:])
                nc.sync.dma_start(out[cols, :], y[:])
            else:
                nc.scalar.copy(y[:], res[:])
                nc.scalar.dma_start(out[cols, :], y[:])
